import numpy as np
import ml_dtypes


def mxq(x, axis, fmt="e4m3"):
    dtype, down = {"e4m3": (ml_dtypes.float8_e4m3fn, 7), "e5m2": (ml_dtypes.float8_e5m2, 14)}[fmt]
    v = np.moveaxis(np.asarray(x, np.float32).astype(ml_dtypes.bfloat16).astype(np.float64), axis, -1)
    blocks = v.reshape(v.shape[:-1] + (-1, 32))
    amax = np.abs(blocks).max(-1, keepdims=True)
    byte = np.maximum(np.where(amax > 0, np.frexp(amax)[1] - 1 + 127, 0) - down, 1)
    scale = np.exp2(byte - 127.0)
    codes = (blocks / scale).astype(np.float32).astype(dtype).astype(np.float64)
    return np.moveaxis((codes * scale).reshape(v.shape), -1, axis)


WIDE = False


def mx_kscale(k):
    if not WIDE:
        return np.ones(k)
    levels = np.array([10, -10, 5, -5, 0])
    if k % 512:
        return np.exp2(np.random.permutation(np.resize(levels, k // 32))).repeat(32)
    a = np.empty((k // 512, 16))
    for p in range(k // 512):
        a[p, :8] = np.random.permutation(np.resize(levels, 8))
        for g in range(8):
            far = levels[np.abs(levels - a[p, g]) >= 10]
            a[p, g + 8] = far[np.random.randint(len(far))]
    return np.exp2(a.ravel()).repeat(32)


def f64(x):
    return np.asarray(x).astype(np.float64)


E2M1 = np.array([0.0, 0.5, 1.0, 1.5, 2.0, 3.0, 4.0, 6.0, -0.0, -0.5, -1.0, -1.5, -2.0, -3.0, -4.0, -6.0])


def pack_weight(w, fmt):
    k, n = w.shape
    w = f64(np.asarray(w, np.float32).astype(ml_dtypes.bfloat16)).reshape(k // 32, 32, n)
    amax = np.abs(w).max(1)
    if fmt == "e4m3":
        byte = np.frexp(amax)[1] - 1 + 127 - 7
    else:
        mant, ex = np.frexp(amax / 6.0)
        byte = np.where(mant > 0.5, ex, ex - 1) + 127
    byte = np.clip(np.where(amax > 0, byte, 1), 1, 254)
    scaled = (w * np.exp2(127.0 - byte)[:, None, :]).reshape(k, n).astype(np.float32)
    by_word = np.ascontiguousarray(scaled.reshape(k // 512, 128, 4, n).transpose(0, 1, 3, 2))
    if fmt == "e4m3":
        words = by_word.astype(ml_dtypes.float8_e4m3fn).view(np.uint8)
    else:
        c = by_word.astype(ml_dtypes.float4_e2m1fn).view(np.uint8) & 0xF
        words = (c[..., 0::2] | (c[..., 1::2] << 4)).reshape(k // 512, 128, 2 * n)
    return np.ascontiguousarray(words), np.ascontiguousarray(byte.astype(np.uint8).reshape(k // 512, 16, n))


def unpack_weight(words, scales, fmt):
    g, _, n = scales.shape
    words = np.ascontiguousarray(words).reshape(g, 128, n, -1)
    if fmt == "e4m3":
        vals = words.view(ml_dtypes.float8_e4m3fn).astype(np.float64)
    else:
        nib = np.empty((g, 128, n, 4), np.uint8)
        nib[..., 0::2] = words & 0xF
        nib[..., 1::2] = words >> 4
        vals = E2M1[nib]
    vals = vals * np.repeat(np.exp2(scales.astype(np.float64) - 127.0), 8, axis=1)[..., None]
    return vals.transpose(0, 1, 3, 2).reshape(g * 512, n)


K, M, T = 1024, 512, 1536


def setup_inputs():
    n = np.random.standard_normal
    s = mx_kscale(K)[:, None]
    x = n((K, T)) * s
    x4 = pack_weight(x, "e2m1")
    rest = x - unpack_weight(*x4, "e2m1")
    p_w4 = pack_weight(n((K, M)) / np.sqrt(K) / s, "e2m1")
    return {
        "x4_words": x4[0],
        "x4_scales": x4[1],
        "xr": (rest).astype(np.float32),
        "w4_words": p_w4[0],
        "w4_scales": p_w4[1],
    }


def reference(x4_words, x4_scales, xr, w4_words, w4_scales):
    x4_ = unpack_weight(x4_words, x4_scales, "e2m1")
    xr_ = mxq(f64(xr), 0, "e4m3")
    w4_ = unpack_weight(w4_words, w4_scales, "e2m1")
    y = x4_.T @ w4_ + xr_.T @ w4_
    return y

@@ -1,0 +1,173 @@
+from contextlib import ExitStack
+
+import concourse.mybir as mybir
+
+K, N, T = 1024, 512, 1536
+FLOPS = 2 * 2 * K * N * T
+
+F32 = mybir.dt.float32
+BF16 = mybir.dt.bfloat16
+I32 = mybir.dt.int32
+U32 = mybir.dt.uint32
+U8 = mybir.dt.uint8
+E4M3X4 = mybir.dt.float8_e4m3fn_x4
+E2M1X4 = mybir.dt.float4_e2m1fn_x4
+
+P = 128
+PACK = 4
+K_PASS = P * PACK
+PASSES = K // K_PASS
+LOADS = ((0, 0, 768), (1, 0, 768), (0, 768, 1536), (1, 768, 1280), (1, 1280, 1536))
+GROUP = 256
+TILES = T // P
+BANKS = 8
+
+
+def tile_mix_xres_tm_none_kernel(tc, x4_words, x4_scales, xr, w4_words, w4_scales, out):
+    nc = tc.nc
+    with ExitStack() as ctx:
+        keep = ctx.enter_context(tc.tile_pool(name="keep", bufs=1))
+        psum = ctx.enter_context(tc.psum_pool(name="psum", bufs=1))
+
+        w_words = keep.tile([P, PASSES * 2 * N], U8, name="w_words", align_bytes=64)
+        x_words = keep.tile([P, PASSES * 2 * T], U8, name="x_words", align_bytes=64)
+        w_scales = keep.tile([P, PASSES * N], U8, name="w_scales", align_bytes=64)
+        x_scales = keep.tile([P, PASSES * T], U8, name="x_scales", align_bytes=64)
+
+        ctx.enter_context(tc.manual_schedule())
+
+        nc.gpsimd.memset(w_scales[:].bitcast(I32), 0)
+        nc.vector.memset(x_scales[:].bitcast(I32), 0)
+
+        raw = {}
+
+        def load_words(tile, rows):
+            nc.sync.dma_start(
+                out=tile[:].rearrange("p (a c) -> p a c", a=PASSES).bitcast(I32),
+                in_=rows.rearrange("a p c -> p a c").bitcast(I32),
+            )
+
+        def load_scales(queue, tile, rows, r):
+            queue.dma_start(
+                out=tile[r:P:32, :].rearrange("q (a c) -> q a c", a=PASSES).bitcast(I32),
+                in_=rows.rearrange("a (q r) c -> r q a c", r=4)[r].bitcast(I32),
+            )
+
+        def load_xr(a, first, end):
+            chunk = keep.tile([P, PACK, end - first], F32, name=f"raw{a}_{first}")
+            nc.sync.dma_start(
+                out=chunk[:],
+                in_=xr[a * K_PASS : (a + 1) * K_PASS, first:end].rearrange("(p j) t -> p j t", j=PACK),
+            )
+            for g in range(first // GROUP, end // GROUP):
+                raw[a, g] = chunk[:, :, g * GROUP - first : (g + 1) * GROUP - first]
+
+        load_words(w_words, w4_words)
+        for r in range(4):
+            load_scales(nc.scalar, w_scales, w4_scales, r)
+        for r in range(2):
+            load_scales(nc.sync, x_scales, x4_scales, r)
+        load_words(x_words, x4_words)
+        for r in range(2, 4):
+            load_scales(nc.sync, x_scales, x4_scales, r)
+        for load in LOADS:
+            load_xr(*load)
+
+        grouped, codes, scales, acc = {}, {}, {}, {}
+
+        def cast(copy, a, g, first=0, end=GROUP):
+            if (a, g) not in grouped:
+                grouped[a, g] = keep.tile([P, GROUP, PACK], BF16, name=f"grouped{a}{g}", align_bytes=64)
+            copy(
+                out=grouped[a, g][:, first:end, :].rearrange("p (b i) j -> p b j i", i=4),
+                in_=raw[a, g][:, :, first:end].rearrange("p j (b i) -> p b j i", i=4),
+            )
+
+        def share(a, g):
+            cast(vec, a, g, 0, P)
+            cast(act, a, g, P, GROUP)
+
+        def quantize(a, g):
+            codes[a, g] = keep.tile([P, GROUP], U32, name=f"codes{a}{g}", align_bytes=64)
+            scales[a, g] = keep.tile([P, GROUP], U8, name=f"scales{a}{g}", align_bytes=64)
+            nc.vector.quantize_mx(
+                out=codes[a, g][:].bitcast(E4M3X4),
+                scales=scales[a, g][:],
+                in_=grouped[a, g][:].rearrange("p t j -> p (t j)"),
+            )
+
+        def multiply(i, a, lhs, lhs_scale, start, stop):
+            nc.tensor.matmul_mx(
+                out=acc[i][:],
+                lhsT=lhs,
+                lhsT_scale=lhs_scale,
+                rhs=w_words[:, a * 2 * N : (a + 1) * 2 * N].bitcast(E2M1X4),
+                rhs_scale=w_scales[:, a * N : (a + 1) * N],
+                start=start,
+                stop=stop,
+            )
+
+        def multiply_x4(i):
+            acc[i] = psum.tile([P, N], F32, name=f"acc{i % BANKS}")
+            for a in range(PASSES):
+                col = a * T + i * P
+                multiply(i, a, x_words[:, 2 * col : 2 * (col + P)].bitcast(E2M1X4), x_scales[:, col : col + P], a == 0, False)
+
+        def multiply_xr(a, g):
+            for h in range(GROUP // P):
+                cols = slice(h * P, (h + 1) * P)
+                multiply(g * (GROUP // P) + h, a, codes[a, g][:, cols].bitcast(E4M3X4), scales[a, g][:, cols], False, a == PASSES - 1)
+
+        def finish(copy, i):
+            result = keep.tile([P, N], F32, name=f"result{i}")
+            copy(out=result[:], in_=acc[i][:])
+            nc.sync.dma_start(out=out[i * P : (i + 1) * P, :], in_=result[:])
+
+        vec, act = nc.vector.tensor_copy, nc.scalar.copy
+
+        for i in range(BANKS):
+            multiply_x4(i)
+
+        cast(vec, 0, 0)
+        cast(vec, 0, 1)
+        quantize(0, 0)
+        share(0, 2)
+        quantize(0, 1)
+        quantize(0, 2)
+        for g in range(3):
+            multiply_xr(0, g)
+
+        for g in range(3):
+            share(1, g)
+        for g in range(3):
+            quantize(1, g)
+        for g in range(3):
+            multiply_xr(1, g)
+        finish(act, 0)
+        finish(vec, 1)
+        finish(act, 2)
+        finish(act, 3)
+
+        cast(vec, 0, 3)
+        share(0, 4)
+        quantize(0, 3)
+        share(0, 5)
+        quantize(0, 4)
+        quantize(0, 5)
+        finish(act, 4)
+        finish(act, 5)
+        for i in range(BANKS, TILES):
+            multiply_x4(i)
+        for g in range(3, 6):
+            multiply_xr(0, g)
+
+        cast(vec, 1, 3)
+        share(1, 4)
+        quantize(1, 3)
+        quantize(1, 4)
+        share(1, 5)
+        quantize(1, 5)
+        for g in range(3, 6):
+            multiply_xr(1, g)
+        for i in range(6, TILES):
+            finish(vec if i in (8, 10) else act, i)

@@ -17,10 +17,10 @@ P = 128
 PACK = 4
 K_PASS = P * PACK
 PASSES = K // K_PASS
-LOADS = ((0, 0, 768), (1, 0, 768), (0, 768, 1536), (1, 768, 1280), (1, 1280, 1536))
-GROUP = 256
 TILES = T // P
 BANKS = 8
+LOADS = ((0, 0, 6), (1, 0, 6), (0, 6, 12), (1, 6, 10), (1, 10, 12))
+GROUP = 2
 
 
 def tile_mix_xres_tm_none_kernel(tc, x4_words, x4_scales, xr, w4_words, w4_scales, out):
@@ -54,13 +54,13 @@ def tile_mix_xres_tm_none_kernel(tc, x4_words, x4_scales, xr, w4_words, w4_scale
             )
 
         def load_xr(a, first, end):
-            chunk = keep.tile([P, PACK, end - first], F32, name=f"raw{a}_{first}")
+            chunk = keep.tile([P, PACK, (end - first) * P], F32, name=f"raw{a}_{first}")
             nc.sync.dma_start(
                 out=chunk[:],
-                in_=xr[a * K_PASS : (a + 1) * K_PASS, first:end].rearrange("(p j) t -> p j t", j=PACK),
+                in_=xr[a * K_PASS : (a + 1) * K_PASS, first * P : end * P].rearrange("(p j) t -> p j t", j=PACK),
             )
-            for g in range(first // GROUP, end // GROUP):
-                raw[a, g] = chunk[:, :, g * GROUP - first : (g + 1) * GROUP - first]
+            for i in range(first, end):
+                raw[a, i] = chunk[:, :, (i - first) * P : (i - first + 1) * P]
 
         load_words(w_words, w4_words)
         for r in range(4):
@@ -70,31 +70,32 @@ def tile_mix_xres_tm_none_kernel(tc, x4_words, x4_scales, xr, w4_words, w4_scale
         load_words(x_words, x4_words)
         for r in range(2, 4):
             load_scales(nc.sync, x_scales, x4_scales, r)
-        for load in LOADS:
-            load_xr(*load)
+        for a, first, end in LOADS:
+            load_xr(a, first, end)
 
         grouped, codes, scales, acc = {}, {}, {}, {}
+        vec, act = nc.vector.tensor_copy, nc.scalar.copy
 
-        def cast(copy, a, g, first=0, end=GROUP):
-            if (a, g) not in grouped:
-                grouped[a, g] = keep.tile([P, GROUP, PACK], BF16, name=f"grouped{a}{g}", align_bytes=64)
+        def cast(copy, a, i, width):
+            first = i - i % width
+            if (a, first) not in grouped:
+                grouped[a, first] = keep.tile([P, width * P, PACK], BF16, name=f"grouped{a}_{first}", align_bytes=64)
             copy(
-                out=grouped[a, g][:, first:end, :].rearrange("p (b i) j -> p b j i", i=4),
-                in_=raw[a, g][:, :, first:end].rearrange("p j (b i) -> p b j i", i=4),
+                out=grouped[a, first][:, (i - first) * P : (i - first + 1) * P, :].rearrange("p (b i) j -> p b j i", i=4),
+                in_=raw[a, i].rearrange("p j (b i) -> p b j i", i=4),
             )
 
-        def share(a, g):
-            cast(vec, a, g, 0, P)
-            cast(act, a, g, P, GROUP)
-
-        def quantize(a, g):
-            codes[a, g] = keep.tile([P, GROUP], U32, name=f"codes{a}{g}", align_bytes=64)
-            scales[a, g] = keep.tile([P, GROUP], U8, name=f"scales{a}{g}", align_bytes=64)
+        def quantize(a, first, width):
+            words = keep.tile([P, width * P], U32, name=f"codes{a}_{first}", align_bytes=64)
+            plane = keep.tile([P, width * P], U8, name=f"scales{a}_{first}", align_bytes=64)
             nc.vector.quantize_mx(
-                out=codes[a, g][:].bitcast(E4M3X4),
-                scales=scales[a, g][:],
-                in_=grouped[a, g][:].rearrange("p t j -> p (t j)"),
+                out=words[:].bitcast(E4M3X4),
+                scales=plane[:],
+                in_=grouped[a, first][:].rearrange("p t j -> p (t j)"),
             )
+            for h in range(width):
+                codes[a, first + h] = words[:, h * P : (h + 1) * P]
+                scales[a, first + h] = plane[:, h * P : (h + 1) * P]
 
         def multiply(i, a, lhs, lhs_scale, start, stop):
             nc.tensor.matmul_mx(
@@ -113,61 +114,85 @@ def tile_mix_xres_tm_none_kernel(tc, x4_words, x4_scales, xr, w4_words, w4_scale
                 col = a * T + i * P
                 multiply(i, a, x_words[:, 2 * col : 2 * (col + P)].bitcast(E2M1X4), x_scales[:, col : col + P], a == 0, False)
 
-        def multiply_xr(a, g):
-            for h in range(GROUP // P):
-                cols = slice(h * P, (h + 1) * P)
-                multiply(g * (GROUP // P) + h, a, codes[a, g][:, cols].bitcast(E4M3X4), scales[a, g][:, cols], False, a == PASSES - 1)
+        def multiply_xr(a, i):
+            multiply(i, a, codes[a, i].bitcast(E4M3X4), scales[a, i], False, a == PASSES - 1)
 
         def finish(copy, i):
             result = keep.tile([P, N], F32, name=f"result{i}")
             copy(out=result[:], in_=acc[i][:])
             nc.sync.dma_start(out=out[i * P : (i + 1) * P, :], in_=result[:])
 
-        vec, act = nc.vector.tensor_copy, nc.scalar.copy
-
         for i in range(BANKS):
             multiply_x4(i)
 
-        cast(vec, 0, 0)
-        cast(vec, 0, 1)
-        quantize(0, 0)
-        share(0, 2)
-        quantize(0, 1)
-        quantize(0, 2)
-        for g in range(3):
-            multiply_xr(0, g)
+        for i in range(0, 6, 2):
+            cast(vec, 0, i, 2)
+            cast(act, 0, i + 1, 2)
+            if i > 0:
+                quantize(0, i - 2, 2)
+        quantize(0, 4, 2)
+        for i in range(6):
+            multiply_xr(0, i)
 
-        for g in range(3):
-            share(1, g)
-        for g in range(3):
-            quantize(1, g)
-        for g in range(3):
-            multiply_xr(1, g)
+        cast(vec, 1, 0, 1)
+        cast(act, 1, 1, 1)
+        cast(vec, 1, 2, 1)
+        cast(act, 1, 3, 1)
+        quantize(1, 0, 1)
+        quantize(1, 1, 1)
+        cast(vec, 1, 4, 1)
+        quantize(1, 2, 1)
+        quantize(1, 3, 1)
+        cast(vec, 1, 5, 1)
+        quantize(1, 4, 1)
+        quantize(1, 5, 1)
+        for i in range(4):
+            multiply_xr(1, i)
         finish(act, 0)
-        finish(vec, 1)
+        finish(act, 1)
+        multiply_x4(8)
+        multiply_xr(1, 4)
+        multiply_xr(1, 5)
         finish(act, 2)
         finish(act, 3)
+        multiply_x4(9)
+        multiply_x4(10)
 
-        cast(vec, 0, 3)
-        share(0, 4)
-        quantize(0, 3)
-        share(0, 5)
-        quantize(0, 4)
-        quantize(0, 5)
+        cast(vec, 0, 6, 2)
+        cast(vec, 0, 7, 2)
+        cast(vec, 0, 8, 2)
+        cast(act, 0, 9, 2)
+        quantize(0, 6, 2)
+        cast(vec, 0, 10, 2)
+        cast(act, 0, 11, 2)
+        quantize(0, 8, 2)
+        multiply_x4(11)
+        for i in range(6, 9):
+            multiply_xr(0, i)
+
+        cast(vec, 1, 6, 1)
+        cast(act, 1, 7, 1)
         finish(act, 4)
         finish(act, 5)
-        for i in range(BANKS, TILES):
-            multiply_x4(i)
-        for g in range(3, 6):
-            multiply_xr(0, g)
-
-        cast(vec, 1, 3)
-        share(1, 4)
-        quantize(1, 3)
-        quantize(1, 4)
-        share(1, 5)
-        quantize(1, 5)
-        for g in range(3, 6):
-            multiply_xr(1, g)
+        quantize(0, 10, 2)
+        quantize(1, 6, 1)
+        cast(vec, 1, 8, 1)
+        quantize(1, 7, 1)
+        cast(vec, 1, 9, 1)
+        quantize(1, 8, 1)
+        cast(vec, 1, 10, 1)
+        quantize(1, 9, 1)
+        cast(vec, 1, 11, 1)
+        quantize(1, 10, 1)
+        quantize(1, 11, 1)
+        multiply_xr(1, 6)
+        multiply_xr(0, 9)
+        multiply_xr(1, 7)
+        multiply_xr(0, 10)
+        multiply_xr(1, 8)
+        multiply_xr(0, 11)
+        multiply_xr(1, 9)
+        multiply_xr(1, 10)
+        multiply_xr(1, 11)
         for i in range(6, TILES):
-            finish(vec if i in (8, 10) else act, i)
+            finish(vec if i in (9, 11) else act, i)

@@ -19,8 +19,9 @@ K_PASS = P * PACK
 PASSES = K // K_PASS
 TILES = T // P
 BANKS = 8
-LOADS = ((0, 0, 6), (1, 0, 6), (0, 6, 12), (1, 6, 10), (1, 10, 12))
-GROUP = 2
+CHUNK = 4
+LOADS = [(a, first, first + CHUNK) for first in range(0, TILES, CHUNK) for a in range(PASSES)]
+STORES = ((0, 4), (4, 8), (8, 9), (9, 11), (11, 12))
 
 
 def tile_mix_xres_tm_none_kernel(tc, x4_words, x4_scales, xr, w4_words, w4_scales, out):
@@ -117,82 +118,41 @@ def tile_mix_xres_tm_none_kernel(tc, x4_words, x4_scales, xr, w4_words, w4_scale
         def multiply_xr(a, i):
             multiply(i, a, codes[a, i].bitcast(E4M3X4), scales[a, i], False, a == PASSES - 1)
 
+        results, emptied = {}, set()
+
         def finish(copy, i):
-            result = keep.tile([P, N], F32, name=f"result{i}")
-            copy(out=result[:], in_=acc[i][:])
-            nc.sync.dma_start(out=out[i * P : (i + 1) * P, :], in_=result[:])
+            first, end = [s for s in STORES if s[0] <= i < s[1]][0]
+            if first not in results:
+                results[first] = keep.tile([P, end - first, N], F32, name=f"result{first}")
+            copy(out=results[first][:, i - first, :], in_=acc[i][:])
+            emptied.add(i)
+            if all(j in emptied for j in range(first, end)):
+                nc.sync.dma_start(
+                    out=out[first * P : end * P, :].rearrange("(i p) n -> p i n", p=P),
+                    in_=results[first][:],
+                )
 
-        for i in range(BANKS):
-            multiply_x4(i)
+        for first in range(0, TILES, CHUNK):
+            tiles = range(first, first + CHUNK)
+            for i in tiles:
+                if i not in acc:
+                    multiply_x4(i)
 
-        for i in range(0, 6, 2):
-            cast(vec, 0, i, 2)
-            cast(act, 0, i + 1, 2)
-            if i > 0:
-                quantize(0, i - 2, 2)
-        quantize(0, 4, 2)
-        for i in range(6):
-            multiply_xr(0, i)
+            for i in tiles:
+                cast(vec, 0, i, 1)
+                if i > first:
+                    quantize(0, i - 1, 1)
+            quantize(0, tiles[-1], 1)
+            for i in tiles:
+                multiply_xr(0, i)
+            if first + CHUNK < TILES:
+                multiply_x4(first + CHUNK)
 
-        cast(vec, 1, 0, 1)
-        cast(act, 1, 1, 1)
-        cast(vec, 1, 2, 1)
-        cast(act, 1, 3, 1)
-        quantize(1, 0, 1)
-        quantize(1, 1, 1)
-        cast(vec, 1, 4, 1)
-        quantize(1, 2, 1)
-        quantize(1, 3, 1)
-        cast(vec, 1, 5, 1)
-        quantize(1, 4, 1)
-        quantize(1, 5, 1)
-        for i in range(4):
-            multiply_xr(1, i)
-        finish(act, 0)
-        finish(act, 1)
-        multiply_x4(8)
-        multiply_xr(1, 4)
-        multiply_xr(1, 5)
-        finish(act, 2)
-        finish(act, 3)
-        multiply_x4(9)
-        multiply_x4(10)
-
-        cast(vec, 0, 6, 2)
-        cast(vec, 0, 7, 2)
-        cast(vec, 0, 8, 2)
-        cast(act, 0, 9, 2)
-        quantize(0, 6, 2)
-        cast(vec, 0, 10, 2)
-        cast(act, 0, 11, 2)
-        quantize(0, 8, 2)
-        multiply_x4(11)
-        for i in range(6, 9):
-            multiply_xr(0, i)
-
-        cast(vec, 1, 6, 1)
-        cast(act, 1, 7, 1)
-        finish(act, 4)
-        finish(act, 5)
-        quantize(0, 10, 2)
-        quantize(1, 6, 1)
-        cast(vec, 1, 8, 1)
-        quantize(1, 7, 1)
-        cast(vec, 1, 9, 1)
-        quantize(1, 8, 1)
-        cast(vec, 1, 10, 1)
-        quantize(1, 9, 1)
-        cast(vec, 1, 11, 1)
-        quantize(1, 10, 1)
-        quantize(1, 11, 1)
-        multiply_xr(1, 6)
-        multiply_xr(0, 9)
-        multiply_xr(1, 7)
-        multiply_xr(0, 10)
-        multiply_xr(1, 8)
-        multiply_xr(0, 11)
-        multiply_xr(1, 9)
-        multiply_xr(1, 10)
-        multiply_xr(1, 11)
-        for i in range(6, TILES):
-            finish(vec if i in (9, 11) else act, i)
+            for i in tiles:
+                cast(act if i % 2 else vec, 1, i, 1)
+            for i in tiles:
+                quantize(1, i, 1)
+            for i in tiles:
+                multiply_xr(1, i)
+            for i in tiles:
+                finish(vec if first + CHUNK == TILES and i % 2 else act, i)

@@ -64,13 +64,13 @@ def tile_mix_xres_tm_none_kernel(tc, x4_words, x4_scales, xr, w4_words, w4_scale
                 raw[a, i] = chunk[:, :, (i - first) * P : (i - first + 1) * P]
 
         load_words(w_words, w4_words)
-        for r in range(4):
-            load_scales(nc.scalar, w_scales, w4_scales, r)
         for r in range(2):
-            load_scales(nc.sync, x_scales, x4_scales, r)
+            load_scales(nc.scalar, w_scales, w4_scales, r)
+        for r in range(4):
+            load_scales(nc.scalar if r % 2 else nc.sync, x_scales, x4_scales, r)
         load_words(x_words, x4_words)
         for r in range(2, 4):
-            load_scales(nc.sync, x_scales, x4_scales, r)
+            load_scales(nc.sync, w_scales, w4_scales, r)
         for a, first, end in LOADS:
             load_xr(a, first, end)
 

@@ -19,9 +19,8 @@ K_PASS = P * PACK
 PASSES = K // K_PASS
 TILES = T // P
 BANKS = 8
-CHUNK = 4
-LOADS = [(a, first, first + CHUNK) for first in range(0, TILES, CHUNK) for a in range(PASSES)]
-STORES = ((0, 4), (4, 8), (8, 9), (9, 11), (11, 12))
+LOADS = ((0, 4), (4, 6), (6, 8), (8, 10), (10, 12))
+STORES = ((0, 6), (6, 9), (9, 12))
 
 
 def tile_mix_xres_tm_none_kernel(tc, x4_words, x4_scales, xr, w4_words, w4_scales, out):
@@ -54,14 +53,14 @@ def tile_mix_xres_tm_none_kernel(tc, x4_words, x4_scales, xr, w4_words, w4_scale
                 in_=rows.rearrange("a (q r) c -> r q a c", r=4)[r].bitcast(I32),
             )
 
-        def load_xr(a, first, end):
-            chunk = keep.tile([P, PACK, (end - first) * P], F32, name=f"raw{a}_{first}")
+        def load_xr(first, end):
+            chunk = keep.tile([P, PACK, PASSES, (end - first) * P], F32, name=f"raw{first}")
             nc.sync.dma_start(
                 out=chunk[:],
-                in_=xr[a * K_PASS : (a + 1) * K_PASS, first * P : end * P].rearrange("(p j) t -> p j t", j=PACK),
+                in_=xr[:, first * P : end * P].rearrange("(a p j) t -> p j a t", a=PASSES, j=PACK),
             )
             for i in range(first, end):
-                raw[a, i] = chunk[:, :, (i - first) * P : (i - first + 1) * P]
+                raw[i] = chunk[:, :, :, (i - first) * P : (i - first + 1) * P]
 
         load_words(w_words, w4_words)
         for r in range(2):
@@ -71,32 +70,29 @@ def tile_mix_xres_tm_none_kernel(tc, x4_words, x4_scales, xr, w4_words, w4_scale
         load_words(x_words, x4_words)
         for r in range(2, 4):
             load_scales(nc.sync, w_scales, w4_scales, r)
-        for a, first, end in LOADS:
-            load_xr(a, first, end)
+        for first, end in LOADS:
+            load_xr(first, end)
 
         grouped, codes, scales, acc = {}, {}, {}, {}
-        vec, act = nc.vector.tensor_copy, nc.scalar.copy
 
-        def cast(copy, a, i, width):
-            first = i - i % width
-            if (a, first) not in grouped:
-                grouped[a, first] = keep.tile([P, width * P, PACK], BF16, name=f"grouped{a}_{first}", align_bytes=64)
+        def cast(copy, i, first_pass, end_pass):
+            if i not in grouped:
+                grouped[i] = keep.tile([P, PASSES, P, PACK], BF16, name=f"grouped{i}", align_bytes=64)
             copy(
-                out=grouped[a, first][:, (i - first) * P : (i - first + 1) * P, :].rearrange("p (b i) j -> p b j i", i=4),
-                in_=raw[a, i].rearrange("p j (b i) -> p b j i", i=4),
+                out=grouped[i][:, first_pass:end_pass].rearrange("p a (b i) j -> p a b j i", i=4),
+                in_=raw[i][:, :, first_pass:end_pass, :].rearrange("p j a (b i) -> p a b j i", i=4),
             )
 
-        def quantize(a, first, width):
-            words = keep.tile([P, width * P], U32, name=f"codes{a}_{first}", align_bytes=64)
-            plane = keep.tile([P, width * P], U8, name=f"scales{a}_{first}", align_bytes=64)
+        def quantize(i, first_pass, end_pass):
+            if i not in codes:
+                codes[i] = keep.tile([P, PASSES * P], U32, name=f"codes{i}", align_bytes=64)
+                scales[i] = keep.tile([P, PASSES * P], U8, name=f"scales{i}", align_bytes=64)
+            cols = slice(first_pass * P, end_pass * P)
             nc.vector.quantize_mx(
-                out=words[:].bitcast(E4M3X4),
-                scales=plane[:],
-                in_=grouped[a, first][:].rearrange("p t j -> p (t j)"),
+                out=codes[i][:, cols].bitcast(E4M3X4),
+                scales=scales[i][:, cols],
+                in_=grouped[i][:, first_pass:end_pass].rearrange("p a t j -> p (a t j)"),
             )
-            for h in range(width):
-                codes[a, first + h] = words[:, h * P : (h + 1) * P]
-                scales[a, first + h] = plane[:, h * P : (h + 1) * P]
 
         def multiply(i, a, lhs, lhs_scale, start, stop):
             nc.tensor.matmul_mx(
@@ -109,50 +105,68 @@ def tile_mix_xres_tm_none_kernel(tc, x4_words, x4_scales, xr, w4_words, w4_scale
                 stop=stop,
             )
 
-        def multiply_x4(i):
-            acc[i] = psum.tile([P, N], F32, name=f"acc{i % BANKS}")
-            for a in range(PASSES):
-                col = a * T + i * P
-                multiply(i, a, x_words[:, 2 * col : 2 * (col + P)].bitcast(E2M1X4), x_scales[:, col : col + P], a == 0, False)
+        def multiply_x4(i, a):
+            if a == 0:
+                acc[i] = psum.tile([P, N], F32, name=f"acc{i % BANKS}")
+            col = a * T + i * P
+            multiply(i, a, x_words[:, 2 * col : 2 * (col + P)].bitcast(E2M1X4), x_scales[:, col : col + P], a == 0, False)
 
-        def multiply_xr(a, i):
-            multiply(i, a, codes[a, i].bitcast(E4M3X4), scales[a, i], False, a == PASSES - 1)
+        def multiply_xr(i, first_pass, end_pass):
+            for a in range(first_pass, end_pass):
+                cols = slice(a * P, (a + 1) * P)
+                multiply(i, a, codes[i][:, cols].bitcast(E4M3X4), scales[i][:, cols], False, a == PASSES - 1)
 
-        results, emptied = {}, set()
+        results = {}
 
         def finish(copy, i):
             first, end = [s for s in STORES if s[0] <= i < s[1]][0]
             if first not in results:
                 results[first] = keep.tile([P, end - first, N], F32, name=f"result{first}")
             copy(out=results[first][:, i - first, :], in_=acc[i][:])
-            emptied.add(i)
-            if all(j in emptied for j in range(first, end)):
+            if i == end - 1:
                 nc.sync.dma_start(
                     out=out[first * P : end * P, :].rearrange("(i p) n -> p i n", p=P),
                     in_=results[first][:],
                 )
 
-        for first in range(0, TILES, CHUNK):
-            tiles = range(first, first + CHUNK)
-            for i in tiles:
-                if i not in acc:
-                    multiply_x4(i)
+        vec, act = nc.vector.tensor_copy, nc.scalar.copy
+        for i in range(BANKS):
+            for a in range(PASSES):
+                multiply_x4(i, a)
 
-            for i in tiles:
-                cast(vec, 0, i, 1)
-                if i > first:
-                    quantize(0, i - 1, 1)
-            quantize(0, tiles[-1], 1)
-            for i in tiles:
-                multiply_xr(0, i)
-            if first + CHUNK < TILES:
-                multiply_x4(first + CHUNK)
+        def close(i, first_pass, end_pass):
+            quantize(i, first_pass, end_pass)
+            multiply_xr(i, first_pass, end_pass)
+            late = i + BANKS - 3
+            if end_pass == PASSES and BANKS <= late < TILES:
+                for a in range(PASSES):
+                    multiply_x4(late, a)
 
-            for i in tiles:
-                cast(act if i % 2 else vec, 1, i, 1)
-            for i in tiles:
-                quantize(1, i, 1)
-            for i in tiles:
-                multiply_xr(1, i)
-            for i in tiles:
-                finish(vec if first + CHUNK == TILES and i % 2 else act, i)
+        for i in range(4):
+            cast(vec if i < 2 else act, i, 0, PASSES)
+        for i in range(4):
+            if i >= 2:
+                finish(act, i - 2)
+            close(i, 0, PASSES)
+
+        for first, end in LOADS[1:]:
+            shared = first >= BANKS
+            if shared:
+                cast(act, first + 1, 0, 1)
+            finish(act, first - 2)
+            finish(act, first - 1)
+            if end < TILES:
+                cast(vec, first, 0, PASSES)
+                cast(vec, first + 1, 1 if shared else 0, PASSES)
+                close(first, 0, PASSES)
+                close(first + 1, 0, PASSES)
+            else:
+                for a in range(PASSES):
+                    cast(vec, first, a, a + 1)
+                for a in range(PASSES):
+                    close(first, a, a + 1)
+                cast(vec, first + 1, 1, 2)
+                for a in range(PASSES):
+                    close(first + 1, a, a + 1)
+        finish(act, TILES - 2)
+        finish(vec, TILES - 1)

@@ -19,8 +19,8 @@ K_PASS = P * PACK
 PASSES = K // K_PASS
 TILES = T // P
 BANKS = 8
-LOADS = ((0, 4), (4, 6), (6, 8), (8, 10), (10, 12))
-STORES = ((0, 6), (6, 9), (9, 12))
+LOADS = ((0, 3), (3, 6), (6, 8), (8, 10), (10, 12))
+STORES = ((0, 5), (5, 8), (8, 10), (10, 12))
 
 
 def tile_mix_xres_tm_none_kernel(tc, x4_words, x4_scales, xr, w4_words, w4_scales, out):
@@ -137,36 +137,34 @@ def tile_mix_xres_tm_none_kernel(tc, x4_words, x4_scales, xr, w4_words, w4_scale
         def close(i, first_pass, end_pass):
             quantize(i, first_pass, end_pass)
             multiply_xr(i, first_pass, end_pass)
-            late = i + BANKS - 3
-            if end_pass == PASSES and BANKS <= late < TILES:
-                for a in range(PASSES):
-                    multiply_x4(late, a)
 
-        for i in range(4):
-            cast(vec if i < 2 else act, i, 0, PASSES)
-        for i in range(4):
-            if i >= 2:
-                finish(act, i - 2)
-            close(i, 0, PASSES)
-
-        for first, end in LOADS[1:]:
-            shared = first >= BANKS
-            if shared:
-                cast(act, first + 1, 0, 1)
-            finish(act, first - 2)
-            finish(act, first - 1)
+        pending = []
+        for chunk, (first, end) in enumerate(LOADS):
+            last = end - 1
+            by_scalar = PASSES if end - first == 3 else 1 if first >= BANKS else 0
+            if by_scalar:
+                cast(act, last, 0, by_scalar)
+            for i in pending:
+                finish(act, i)
             if end < TILES:
-                cast(vec, first, 0, PASSES)
-                cast(vec, first + 1, 1 if shared else 0, PASSES)
-                close(first, 0, PASSES)
-                close(first + 1, 0, PASSES)
+                for i in range(first, last):
+                    cast(vec, i, 0, PASSES)
+                if by_scalar < PASSES:
+                    cast(vec, last, by_scalar, PASSES)
+                for i in range(first, end):
+                    close(i, 0, PASSES)
+                    if i == first and end - first == 3:
+                        finish(act, first)
+                for a in range(PASSES):
+                    multiply_x4(BANKS + chunk, a)
             else:
                 for a in range(PASSES):
                     cast(vec, first, a, a + 1)
                 for a in range(PASSES):
                     close(first, a, a + 1)
-                cast(vec, first + 1, 1, 2)
+                cast(vec, last, 1, PASSES)
                 for a in range(PASSES):
-                    close(first + 1, a, a + 1)
+                    close(last, a, a + 1)
+            pending = [last - 1, last]
         finish(act, TILES - 2)
         finish(vec, TILES - 1)

@@ -19,8 +19,8 @@ K_PASS = P * PACK
 PASSES = K // K_PASS
 TILES = T // P
 BANKS = 8
-LOADS = ((0, 3), (3, 6), (6, 8), (8, 10), (10, 12))
-STORES = ((0, 5), (5, 8), (8, 10), (10, 12))
+LOADS = ((0, 1, 0, 5), (1, 2, 0, 8), (0, 1, 5, 12), (1, 2, 8, 12))
+STORES = ((0, 4), (4, 6), (6, 8), (8, 9), (9, 10), (10, 11), (11, 12))
 
 
 def tile_mix_xres_tm_none_kernel(tc, x4_words, x4_scales, xr, w4_words, w4_scales, out):
@@ -53,14 +53,14 @@ def tile_mix_xres_tm_none_kernel(tc, x4_words, x4_scales, xr, w4_words, w4_scale
                 in_=rows.rearrange("a (q r) c -> r q a c", r=4)[r].bitcast(I32),
             )
 
-        def load_xr(first, end):
-            chunk = keep.tile([P, PACK, PASSES, (end - first) * P], F32, name=f"raw{first}")
-            nc.sync.dma_start(
-                out=chunk[:],
-                in_=xr[:, first * P : end * P].rearrange("(a p j) t -> p j a t", a=PASSES, j=PACK),
-            )
-            for i in range(first, end):
-                raw[i] = chunk[:, :, :, (i - first) * P : (i - first + 1) * P]
+        def load_xr(first_pass, end_pass, first, end):
+            passes = end_pass - first_pass
+            chunk = keep.tile([P, PACK, passes, (end - first) * P], F32, name=f"raw{first_pass}_{first}")
+            rows = xr[first_pass * K_PASS : end_pass * K_PASS, first * P : end * P]
+            nc.sync.dma_start(out=chunk[:], in_=rows.rearrange("(a p j) t -> p j a t", a=passes, j=PACK))
+            for a in range(first_pass, end_pass):
+                for i in range(first, end):
+                    raw[a, i] = (chunk, a - first_pass, i - first)
 
         load_words(w_words, w4_words)
         for r in range(2):
@@ -70,29 +70,41 @@ def tile_mix_xres_tm_none_kernel(tc, x4_words, x4_scales, xr, w4_words, w4_scale
         load_words(x_words, x4_words)
         for r in range(2, 4):
             load_scales(nc.sync, w_scales, w4_scales, r)
-        for first, end in LOADS:
-            load_xr(first, end)
+        for load in LOADS:
+            load_xr(*load)
 
         grouped, codes, scales, acc = {}, {}, {}, {}
 
-        def cast(copy, i, first_pass, end_pass):
-            if i not in grouped:
-                grouped[i] = keep.tile([P, PASSES, P, PACK], BF16, name=f"grouped{i}", align_bytes=64)
+        def group(first_pass, end_pass, first, end):
+            shape = [P, end_pass - first_pass, (end - first) * P]
+            tile = keep.tile(shape + [PACK], BF16, name=f"grouped{first_pass}_{first}", align_bytes=64)
+            grouped[first_pass, first] = (tile, end_pass, end)
+
+        def cast(copy, first_pass, end_pass, first, end):
+            group(first_pass, end_pass, first, end)
+            chunk, a, i = raw[first_pass, first]
             copy(
-                out=grouped[i][:, first_pass:end_pass].rearrange("p a (b i) j -> p a b j i", i=4),
-                in_=raw[i][:, :, first_pass:end_pass, :].rearrange("p j a (b i) -> p a b j i", i=4),
+                out=grouped[first_pass, first][0][:].rearrange("p a (b i) j -> p a b j i", i=4),
+                in_=chunk[:, :, a : a + end_pass - first_pass, i * P : (i + end - first) * P].rearrange(
+                    "p j a (b i) -> p a b j i", i=4
+                ),
             )
 
-        def quantize(i, first_pass, end_pass):
-            if i not in codes:
-                codes[i] = keep.tile([P, PASSES * P], U32, name=f"codes{i}", align_bytes=64)
-                scales[i] = keep.tile([P, PASSES * P], U8, name=f"scales{i}", align_bytes=64)
-            cols = slice(first_pass * P, end_pass * P)
+        def quantize(first_pass, first):
+            tile, end_pass, end = grouped[first_pass, first]
+            width = (end - first) * P
+            words = keep.tile([P, (end_pass - first_pass) * width], U32, name=f"codes{first_pass}_{first}", align_bytes=64)
+            plane = keep.tile([P, (end_pass - first_pass) * width], U8, name=f"scales{first_pass}_{first}", align_bytes=64)
             nc.vector.quantize_mx(
-                out=codes[i][:, cols].bitcast(E4M3X4),
-                scales=scales[i][:, cols],
-                in_=grouped[i][:, first_pass:end_pass].rearrange("p a t j -> p (a t j)"),
+                out=words[:].bitcast(E4M3X4),
+                scales=plane[:],
+                in_=tile[:].rearrange("p a t j -> p (a t j)"),
             )
+            for a in range(first_pass, end_pass):
+                for i in range(first, end):
+                    col = (a - first_pass) * width + (i - first) * P
+                    codes[a, i] = words[:, col : col + P]
+                    scales[a, i] = plane[:, col : col + P]
 
         def multiply(i, a, lhs, lhs_scale, start, stop):
             nc.tensor.matmul_mx(
@@ -111,10 +123,11 @@ def tile_mix_xres_tm_none_kernel(tc, x4_words, x4_scales, xr, w4_words, w4_scale
             col = a * T + i * P
             multiply(i, a, x_words[:, 2 * col : 2 * (col + P)].bitcast(E2M1X4), x_scales[:, col : col + P], a == 0, False)
 
-        def multiply_xr(i, first_pass, end_pass):
-            for a in range(first_pass, end_pass):
-                cols = slice(a * P, (a + 1) * P)
-                multiply(i, a, codes[i][:, cols].bitcast(E4M3X4), scales[i][:, cols], False, a == PASSES - 1)
+        done = {i: 0 for i in range(TILES)}
+
+        def multiply_xr(a, i):
+            done[i] = done[i] + 1
+            multiply(i, a, codes[a, i].bitcast(E4M3X4), scales[a, i], False, done[i] == PASSES)
 
         results = {}
 
@@ -130,41 +143,69 @@ def tile_mix_xres_tm_none_kernel(tc, x4_words, x4_scales, xr, w4_words, w4_scale
                 )
 
         vec, act = nc.vector.tensor_copy, nc.scalar.copy
-        for i in range(BANKS):
+
+        def open_with_x4(i):
             for a in range(PASSES):
                 multiply_x4(i, a)
 
-        def close(i, first_pass, end_pass):
-            quantize(i, first_pass, end_pass)
-            multiply_xr(i, first_pass, end_pass)
+        def close(a, i):
+            quantize(a, i)
+            multiply_xr(a, i)
 
-        pending = []
-        for chunk, (first, end) in enumerate(LOADS):
-            last = end - 1
-            by_scalar = PASSES if end - first == 3 else 1 if first >= BANKS else 0
-            if by_scalar:
-                cast(act, last, 0, by_scalar)
-            for i in pending:
-                finish(act, i)
-            if end < TILES:
-                for i in range(first, last):
-                    cast(vec, i, 0, PASSES)
-                if by_scalar < PASSES:
-                    cast(vec, last, by_scalar, PASSES)
-                for i in range(first, end):
-                    close(i, 0, PASSES)
-                    if i == first and end - first == 3:
-                        finish(act, first)
-                for a in range(PASSES):
-                    multiply_x4(BANKS + chunk, a)
-            else:
-                for a in range(PASSES):
-                    cast(vec, first, a, a + 1)
-                for a in range(PASSES):
-                    close(first, a, a + 1)
-                cast(vec, last, 1, PASSES)
-                for a in range(PASSES):
-                    close(last, a, a + 1)
-            pending = [last - 1, last]
-        finish(act, TILES - 2)
-        finish(vec, TILES - 1)
+        def pair(a, first, end):
+            quantize(a, first)
+            for i in range(first, end):
+                multiply_xr(a, i)
+
+        for i in range(BANKS):
+            open_with_x4(i)
+
+        cast(vec, 0, 1, 0, 2)
+        cast(vec, 0, 1, 2, 4)
+        cast(act, 0, 1, 4, 5)
+        pair(0, 0, 2)
+        pair(0, 2, 4)
+        pair(0, 4, 5)
+
+        for i in range(4):
+            cast(act if i % 2 else vec, 1, 2, i, i + 1)
+        close(1, 0)
+        close(1, 1)
+        cast(vec, 1, 2, 4, 5)
+        for i in range(2, 5):
+            close(1, i)
+        for i in range(4):
+            finish(act, i)
+        open_with_x4(8)
+        open_with_x4(9)
+        cast(vec, 1, 2, 5, 7)
+        cast(vec, 1, 2, 7, 8)
+        pair(1, 5, 7)
+        pair(1, 7, 8)
+        finish(vec, 4)
+
+        for i in range(5, 9):
+            cast(vec if i % 2 else act, 0, 1, i, i + 1)
+        for i in range(5, 8):
+            close(0, i)
+        for i in range(5, 8):
+            finish(act, i)
+        cast(vec, 0, 1, 9, 10)
+        cast(vec, 0, 1, 10, 12)
+        open_with_x4(10)
+        close(0, 8)
+        close(0, 9)
+        open_with_x4(11)
+
+        cast(vec, 1, 2, 8, 9)
+        cast(vec, 1, 2, 9, 10)
+        cast(act, 1, 2, 11, 12)
+        close(1, 8)
+        close(1, 9)
+        cast(vec, 1, 2, 10, 11)
+        quantize(0, 10)
+        for i in (10, 11):
+            multiply_xr(0, i)
+            close(1, i)
+        for i in range(8, TILES):
+            finish(vec if i % 2 else act, i)

@@ -19,8 +19,8 @@ K_PASS = P * PACK
 PASSES = K // K_PASS
 TILES = T // P
 BANKS = 8
-LOADS = ((0, 1, 0, 5), (1, 2, 0, 8), (0, 1, 5, 12), (1, 2, 8, 12))
-STORES = ((0, 4), (4, 6), (6, 8), (8, 9), (9, 10), (10, 11), (11, 12))
+LOADS = ((0, 1, 0, 8), (1, 2, 0, 4), (1, 2, 4, 8), (1, 2, 8, 12), (0, 1, 8, 12))
+STORES = ((0, 4), (4, 8), (8, 9), (9, 10), (10, 11), (11, 12))
 
 
 def tile_mix_xres_tm_none_kernel(tc, x4_words, x4_scales, xr, w4_words, w4_scales, out):
@@ -152,60 +152,48 @@ def tile_mix_xres_tm_none_kernel(tc, x4_words, x4_scales, xr, w4_words, w4_scale
             quantize(a, i)
             multiply_xr(a, i)
 
-        def pair(a, first, end):
+        def pair(a, first):
             quantize(a, first)
-            for i in range(first, end):
-                multiply_xr(a, i)
+            multiply_xr(a, first)
+            multiply_xr(a, first + 1)
 
         for i in range(BANKS):
             open_with_x4(i)
 
-        cast(vec, 0, 1, 0, 2)
-        cast(vec, 0, 1, 2, 4)
-        cast(act, 0, 1, 4, 5)
-        pair(0, 0, 2)
-        pair(0, 2, 4)
-        pair(0, 4, 5)
+        for first in range(0, 8, 2):
+            cast(vec if first < 4 else act, 0, 1, first, first + 2)
+        pair(0, 0)
+        pair(0, 2)
 
         for i in range(4):
             cast(act if i % 2 else vec, 1, 2, i, i + 1)
-        close(1, 0)
-        close(1, 1)
-        cast(vec, 1, 2, 4, 5)
-        for i in range(2, 5):
+        for i in range(4):
             close(1, i)
         for i in range(4):
             finish(act, i)
-        open_with_x4(8)
-        open_with_x4(9)
-        cast(vec, 1, 2, 5, 7)
-        cast(vec, 1, 2, 7, 8)
-        pair(1, 5, 7)
-        pair(1, 7, 8)
-        finish(vec, 4)
+        pair(0, 4)
+        pair(0, 6)
 
-        for i in range(5, 9):
-            cast(vec if i % 2 else act, 0, 1, i, i + 1)
-        for i in range(5, 8):
-            close(0, i)
-        for i in range(5, 8):
-            finish(act, i)
-        cast(vec, 0, 1, 9, 10)
-        cast(vec, 0, 1, 10, 12)
-        open_with_x4(10)
-        close(0, 8)
-        close(0, 9)
-        open_with_x4(11)
-
-        cast(vec, 1, 2, 8, 9)
-        cast(vec, 1, 2, 9, 10)
-        cast(act, 1, 2, 11, 12)
-        close(1, 8)
-        close(1, 9)
-        cast(vec, 1, 2, 10, 11)
-        quantize(0, 10)
-        for i in (10, 11):
-            multiply_xr(0, i)
+        cast(vec, 1, 2, 4, 5)
+        for i in range(4, 8):
+            if i < 7:
+                cast(vec, 1, 2, i + 1, i + 2)
             close(1, i)
+            if i == 5:
+                open_with_x4(8)
+        for i in range(4, 8):
+            finish(act, i)
+        for i in range(9, TILES):
+            open_with_x4(i)
+
+        cast(vec, 1, 2, 8, 10)
+        cast(vec, 1, 2, 10, 12)
+        pair(1, 8)
+        pair(1, 10)
+
+        for i in range(8, TILES):
+            cast(act if i % 2 else vec, 0, 1, i, i + 1)
+        for i in range(8, TILES):
+            close(0, i)
         for i in range(8, TILES):
             finish(vec if i % 2 else act, i)

from contextlib import ExitStack

import concourse.mybir as mybir

K, N, T = 1024, 512, 1536
FLOPS = 2 * 2 * K * N * T

F32 = mybir.dt.float32
BF16 = mybir.dt.bfloat16
I32 = mybir.dt.int32
U32 = mybir.dt.uint32
U8 = mybir.dt.uint8
E4M3X4 = mybir.dt.float8_e4m3fn_x4
E2M1X4 = mybir.dt.float4_e2m1fn_x4

P = 128
PACK = 4
K_PASS = P * PACK
PASSES = K // K_PASS
TILES = T // P
BANKS = 8
LOADS = ((0, 1, 0, 8), (1, 2, 0, 4), (1, 2, 4, 8), (1, 2, 8, 12), (0, 1, 8, 12))
STORES = ((0, 4), (4, 8), (8, 9), (9, 10), (10, 11), (11, 12))


def tile_mix_xres_tm_none_kernel(tc, x4_words, x4_scales, xr, w4_words, w4_scales, out):
    nc = tc.nc
    with ExitStack() as ctx:
        keep = ctx.enter_context(tc.tile_pool(name="keep", bufs=1))
        psum = ctx.enter_context(tc.psum_pool(name="psum", bufs=1))

        w_words = keep.tile([P, PASSES * 2 * N], U8, name="w_words", align_bytes=64)
        x_words = keep.tile([P, PASSES * 2 * T], U8, name="x_words", align_bytes=64)
        w_scales = keep.tile([P, PASSES * N], U8, name="w_scales", align_bytes=64)
        x_scales = keep.tile([P, PASSES * T], U8, name="x_scales", align_bytes=64)

        ctx.enter_context(tc.manual_schedule())

        nc.gpsimd.memset(w_scales[:].bitcast(I32), 0)
        nc.vector.memset(x_scales[:].bitcast(I32), 0)

        raw = {}

        def load_words(tile, rows):
            nc.sync.dma_start(
                out=tile[:].rearrange("p (a c) -> p a c", a=PASSES).bitcast(I32),
                in_=rows.rearrange("a p c -> p a c").bitcast(I32),
            )

        def load_scales(queue, tile, rows, r):
            queue.dma_start(
                out=tile[r:P:32, :].rearrange("q (a c) -> q a c", a=PASSES).bitcast(I32),
                in_=rows.rearrange("a (q r) c -> r q a c", r=4)[r].bitcast(I32),
            )

        def load_xr(first_pass, end_pass, first, end):
            passes = end_pass - first_pass
            chunk = keep.tile([P, PACK, passes, (end - first) * P], F32, name=f"raw{first_pass}_{first}")
            rows = xr[first_pass * K_PASS : end_pass * K_PASS, first * P : end * P]
            nc.sync.dma_start(out=chunk[:], in_=rows.rearrange("(a p j) t -> p j a t", a=passes, j=PACK))
            for a in range(first_pass, end_pass):
                for i in range(first, end):
                    raw[a, i] = (chunk, a - first_pass, i - first)

        load_words(w_words, w4_words)
        for r in range(2):
            load_scales(nc.scalar, w_scales, w4_scales, r)
        for r in range(4):
            load_scales(nc.scalar if r % 2 else nc.sync, x_scales, x4_scales, r)
        load_words(x_words, x4_words)
        for r in range(2, 4):
            load_scales(nc.sync, w_scales, w4_scales, r)
        for load in LOADS:
            load_xr(*load)

        grouped, codes, scales, acc = {}, {}, {}, {}

        def group(first_pass, end_pass, first, end):
            shape = [P, end_pass - first_pass, (end - first) * P]
            tile = keep.tile(shape + [PACK], BF16, name=f"grouped{first_pass}_{first}", align_bytes=64)
            grouped[first_pass, first] = (tile, end_pass, end)

        def cast(copy, first_pass, end_pass, first, end):
            group(first_pass, end_pass, first, end)
            chunk, a, i = raw[first_pass, first]
            copy(
                out=grouped[first_pass, first][0][:].rearrange("p a (b i) j -> p a b j i", i=4),
                in_=chunk[:, :, a : a + end_pass - first_pass, i * P : (i + end - first) * P].rearrange(
                    "p j a (b i) -> p a b j i", i=4
                ),
            )

        def quantize(first_pass, first):
            tile, end_pass, end = grouped[first_pass, first]
            width = (end - first) * P
            words = keep.tile([P, (end_pass - first_pass) * width], U32, name=f"codes{first_pass}_{first}", align_bytes=64)
            plane = keep.tile([P, (end_pass - first_pass) * width], U8, name=f"scales{first_pass}_{first}", align_bytes=64)
            nc.vector.quantize_mx(
                out=words[:].bitcast(E4M3X4),
                scales=plane[:],
                in_=tile[:].rearrange("p a t j -> p (a t j)"),
            )
            for a in range(first_pass, end_pass):
                for i in range(first, end):
                    col = (a - first_pass) * width + (i - first) * P
                    codes[a, i] = words[:, col : col + P]
                    scales[a, i] = plane[:, col : col + P]

        def multiply(i, a, lhs, lhs_scale, start, stop):
            nc.tensor.matmul_mx(
                out=acc[i][:],
                lhsT=lhs,
                lhsT_scale=lhs_scale,
                rhs=w_words[:, a * 2 * N : (a + 1) * 2 * N].bitcast(E2M1X4),
                rhs_scale=w_scales[:, a * N : (a + 1) * N],
                start=start,
                stop=stop,
            )

        def multiply_x4(i, a):
            if a == 0:
                acc[i] = psum.tile([P, N], F32, name=f"acc{i % BANKS}")
            col = a * T + i * P
            multiply(i, a, x_words[:, 2 * col : 2 * (col + P)].bitcast(E2M1X4), x_scales[:, col : col + P], a == 0, False)

        done = {i: 0 for i in range(TILES)}

        def multiply_xr(a, i):
            done[i] = done[i] + 1
            multiply(i, a, codes[a, i].bitcast(E4M3X4), scales[a, i], False, done[i] == PASSES)

        results = {}

        def finish(copy, i):
            first, end = [s for s in STORES if s[0] <= i < s[1]][0]
            if first not in results:
                results[first] = keep.tile([P, end - first, N], F32, name=f"result{first}")
            copy(out=results[first][:, i - first, :], in_=acc[i][:])
            if i == end - 1:
                nc.sync.dma_start(
                    out=out[first * P : end * P, :].rearrange("(i p) n -> p i n", p=P),
                    in_=results[first][:],
                )

        vec, act = nc.vector.tensor_copy, nc.scalar.copy

        def open_with_x4(i):
            for a in range(PASSES):
                multiply_x4(i, a)

        def close(a, i):
            quantize(a, i)
            multiply_xr(a, i)

        def pair(a, first):
            quantize(a, first)
            multiply_xr(a, first)
            multiply_xr(a, first + 1)

        for i in range(BANKS):
            open_with_x4(i)

        for first in range(0, 8, 2):
            cast(vec if first < 4 else act, 0, 1, first, first + 2)
        pair(0, 0)
        pair(0, 2)

        for i in range(4):
            cast(act if i % 2 else vec, 1, 2, i, i + 1)
        for i in range(4):
            close(1, i)
        for i in range(4):
            finish(act, i)
        pair(0, 4)
        pair(0, 6)

        cast(vec, 1, 2, 4, 5)
        for i in range(4, 8):
            if i < 7:
                cast(vec, 1, 2, i + 1, i + 2)
            close(1, i)
            if i == 5:
                open_with_x4(8)
        for i in range(4, 8):
            finish(act, i)
        for i in range(9, TILES):
            open_with_x4(i)

        cast(vec, 1, 2, 8, 10)
        cast(vec, 1, 2, 10, 12)
        pair(1, 8)
        pair(1, 10)

        for i in range(8, TILES):
            cast(act if i % 2 else vec, 0, 1, i, i + 1)
        for i in range(8, TILES):
            close(0, i)
        for i in range(8, TILES):
            finish(vec if i % 2 else act, i)
